import numpy as np
import ml_dtypes


def mxq(x, axis, fmt="e4m3"):
    dtype, down = {"e4m3": (ml_dtypes.float8_e4m3fn, 7), "e5m2": (ml_dtypes.float8_e5m2, 14)}[fmt]
    v = np.moveaxis(np.asarray(x, np.float32).astype(ml_dtypes.bfloat16).astype(np.float64), axis, -1)
    blocks = v.reshape(v.shape[:-1] + (-1, 32))
    amax = np.abs(blocks).max(-1, keepdims=True)
    byte = np.maximum(np.where(amax > 0, np.frexp(amax)[1] - 1 + 127, 0) - down, 1)
    scale = np.exp2(byte - 127.0)
    codes = (blocks / scale).astype(np.float32).astype(dtype).astype(np.float64)
    return np.moveaxis((codes * scale).reshape(v.shape), -1, axis)


WIDE = False


def mx_kscale(k):
    if not WIDE:
        return np.ones(k)
    levels = np.array([10, -10, 5, -5, 0])
    if k % 512:
        return np.exp2(np.random.permutation(np.resize(levels, k // 32))).repeat(32)
    a = np.empty((k // 512, 16))
    for p in range(k // 512):
        a[p, :8] = np.random.permutation(np.resize(levels, 8))
        for g in range(8):
            far = levels[np.abs(levels - a[p, g]) >= 10]
            a[p, g + 8] = far[np.random.randint(len(far))]
    return np.exp2(a.ravel()).repeat(32)


def f64(x):
    return np.asarray(x).astype(np.float64)


def striped(idx):
    return np.tile(np.asarray(idx).reshape(-1, 16).T, (8, 1)).astype(np.uint16)


def unstriped(offs):
    return offs[:16].T.reshape(-1).astype(np.int64)


E2M1 = np.array([0.0, 0.5, 1.0, 1.5, 2.0, 3.0, 4.0, 6.0, -0.0, -0.5, -1.0, -1.5, -2.0, -3.0, -4.0, -6.0])


def pack_weight(w, fmt):
    k, n = w.shape
    w = f64(np.asarray(w, np.float32).astype(ml_dtypes.bfloat16)).reshape(k // 32, 32, n)
    amax = np.abs(w).max(1)
    if fmt == "e4m3":
        byte = np.frexp(amax)[1] - 1 + 127 - 7
    else:
        mant, ex = np.frexp(amax / 6.0)
        byte = np.where(mant > 0.5, ex, ex - 1) + 127
    byte = np.clip(np.where(amax > 0, byte, 1), 1, 254)
    scaled = (w * np.exp2(127.0 - byte)[:, None, :]).reshape(k, n).astype(np.float32)
    by_word = np.ascontiguousarray(scaled.reshape(k // 512, 128, 4, n).transpose(0, 1, 3, 2))
    if fmt == "e4m3":
        words = by_word.astype(ml_dtypes.float8_e4m3fn).view(np.uint8)
    else:
        c = by_word.astype(ml_dtypes.float4_e2m1fn).view(np.uint8) & 0xF
        words = (c[..., 0::2] | (c[..., 1::2] << 4)).reshape(k // 512, 128, 2 * n)
    return np.ascontiguousarray(words), np.ascontiguousarray(byte.astype(np.uint8).reshape(k // 512, 16, n))


def unpack_weight(words, scales, fmt):
    g, _, n = scales.shape
    words = np.ascontiguousarray(words).reshape(g, 128, n, -1)
    if fmt == "e4m3":
        vals = words.view(ml_dtypes.float8_e4m3fn).astype(np.float64)
    else:
        nib = np.empty((g, 128, n, 4), np.uint8)
        nib[..., 0::2] = words & 0xF
        nib[..., 1::2] = words >> 4
        vals = E2M1[nib]
    vals = vals * np.repeat(np.exp2(scales.astype(np.float64) - 127.0), 8, axis=1)[..., None]
    return vals.transpose(0, 1, 3, 2).reshape(g * 512, n)


K, L, T, C, J = 512, 512, 256, 1024, 512


def setup_inputs():
    n = np.random.standard_normal
    idx = np.random.permutation(C)[:J]
    idx2 = np.random.permutation(C)[:J]
    fk = mx_kscale(K)
    fl = mx_kscale(L)
    wcp = pack_weight(n((K, C)) * 1 / np.sqrt(K) * fk[:, None], "e2m1")
    xsp = pack_weight(n((L, T)) / fl[:, None], "e4m3")
    wsp = pack_weight(n((L, J)) * 1 / np.sqrt(L) * fl[:, None], "e2m1")
    return {
        "xt": (n((K, T)) / fk[:, None]).astype(np.float32),
        "wc_words": wcp[0],
        "wc_scales": wcp[1],
        "xs_words": xsp[0],
        "xs_scales": xsp[1],
        "ws_words": wsp[0],
        "ws_scales": wsp[1],
        "offs": striped(idx),
        "offs2": striped(idx2),
    }


def reference(xt, wc_words, wc_scales, xs_words, xs_scales, ws_words, ws_scales, offs, offs2):
    idx = unstriped(offs)
    idx2 = unstriped(offs2)
    wcu = unpack_weight(wc_words, wc_scales, "e2m1")
    xsu = unpack_weight(xs_words, xs_scales, "e4m3")
    wsu = unpack_weight(ws_words, ws_scales, "e2m1")
    xtq = mxq(f64(xt), 0, "e4m3")
    z = xtq.T @ wcu
    s = xsu.T @ wsu
    y = np.tanh(z[:, idx] - z[:, idx2]) + 0.5 * s
    return y

@@ -1,0 +1,139 @@
+from contextlib import ExitStack
+
+import concourse.mybir as mybir
+
+K, L, T, C, J = 512, 512, 256, 1024, 512
+FLOPS = 2 * K * T * C + 2 * L * T * J
+
+F32 = mybir.dt.float32
+BF16 = mybir.dt.bfloat16
+I32 = mybir.dt.int32
+U32 = mybir.dt.uint32
+U16 = mybir.dt.uint16
+U8 = mybir.dt.uint8
+FP8X4 = mybir.dt.float8_e4m3fn_x4
+FP4X4 = mybir.dt.float4_e2m1fn_x4
+ALU = mybir.AluOpType
+ACT = mybir.ActivationFunctionType
+
+P = 128
+PACK = 4
+BANK = 512
+PIECE = 256
+LANES = 16
+
+
+def load_scales(engines, plane, scales):
+    for q in range(4):
+        engines[q % len(engines)].dma_start(out=plane[32 * q : 32 * q + 4, :].bitcast(I32), in_=scales[0, 4 * q : 4 * q + 4, :].bitcast(I32))
+
+
+def tile_list_class_and_its_rival_kernel(tc, xt, wc_words, wc_scales, xs_words, xs_scales, ws_words, ws_scales, offs, offs2, out):
+    nc = tc.nc
+    tiles = T // P
+    with ExitStack() as ctx:
+        sb = ctx.enter_context(tc.tile_pool(name="sb", bufs=1))
+        ps = ctx.enter_context(tc.psum_pool(name="ps", bufs=1))
+
+        idx = sb.tile([P, J // LANES], U16, name="idx")
+        idx2 = sb.tile([P, J // LANES], U16, name="idx2")
+        wc = [sb.tile([P, 2 * BANK], U8, name=f"wc{h}", align_bytes=64) for h in range(C // BANK)]
+        wc_plane = sb.tile([P, C], U8, name="wc_plane", align_bytes=64)
+        xs = sb.tile([P, T], U32, name="xs", align_bytes=64)
+        ws = sb.tile([P, 2 * J], U8, name="ws", align_bytes=64)
+        xs_plane = sb.tile([P, T], U8, name="xs_plane", align_bytes=64)
+        ws_plane = sb.tile([P, J], U8, name="ws_plane", align_bytes=64)
+        raw = [sb.tile([P, PACK, P], F32, name=f"raw{i}") for i in range(tiles)]
+        woven = [sb.tile([P, P, PACK], BF16, name=f"woven{i}", align_bytes=64) for i in range(tiles)]
+        xq = [sb.tile([P, P], U32, name=f"xq{i}", align_bytes=64) for i in range(tiles)]
+        xq_plane = [sb.tile([P, P], U8, name=f"xq_plane{i}", align_bytes=64) for i in range(tiles)]
+        z = [sb.tile([P, C], F32, name=f"z{i}") for i in range(tiles)]
+        rival = [sb.tile([P, J], F32, name=f"rival{i}") for i in range(tiles)]
+        margin = [sb.tile([P, J], F32, name=f"margin{i}") for i in range(tiles)]
+        bent = [sb.tile([P, J], F32, name=f"bent{i}") for i in range(tiles)]
+        res = [sb.tile([P, J], F32, name=f"res{i}") for i in range(tiles)]
+        widths = [256, 512]
+        z_ps = [[ps.tile([P, widths[i]], F32, name=f"z_ps{i}_{h}") for h in range(C // widths[i])] for i in range(tiles)]
+        s_ps = [ps.tile([P, J], F32, name=f"s_ps{i}") for i in range(tiles)]
+
+        x_rows = xt.rearrange("(p j) t -> p j t", j=PACK)
+        nc.vector.memset(wc_plane[:].bitcast(I32), 0)
+        nc.vector.memset(ws_plane[:].bitcast(I32), 0)
+        nc.vector.memset(xs_plane[:].bitcast(I32), 0)
+        wc_rows = wc_words[0].bitcast(I32)
+        nc.sync.dma_start(out=raw[0][:], in_=x_rows[:, :, 0:P])
+        load_scales([nc.scalar, nc.sync], wc_plane, wc_scales)
+        nc.sync.dma_start(out=wc[0][:].bitcast(I32), in_=wc_rows[:, 0 : BANK // 2])
+        nc.sync.dma_start(out=raw[1][:], in_=x_rows[:, :, P : 2 * P])
+        nc.sync.dma_start(out=wc[1][:].bitcast(I32), in_=wc_rows[:, BANK // 2 : BANK])
+        nc.sync.dma_start(idx2[:], offs2)
+        nc.sync.dma_start(idx[:], offs)
+        nc.sync.dma_start(out=ws[:].bitcast(I32), in_=ws_words[0].bitcast(I32))
+        nc.sync.dma_start(out=xs[:].bitcast(I32), in_=xs_words[0].rearrange("p c r -> p (c r)").bitcast(I32))
+        load_scales([nc.sync], ws_plane, ws_scales)
+        load_scales([nc.sync], xs_plane, xs_scales)
+
+        for i in range(tiles):
+            halves = [slice(0, P // 2), slice(P // 2, P)] if i == 0 else [slice(0, P)]
+            for tok in halves:
+                nc.vector.tensor_copy(
+                    out=woven[i][:, tok, :].rearrange("p (c e) j -> p c j e", e=4),
+                    in_=raw[i][:, :, tok].rearrange("p j (c e) -> p c j e", e=4),
+                )
+            for tok in halves:
+                nc.vector.quantize_mx(
+                    out=xq[i][:, tok].bitcast(FP8X4), scales=xq_plane[i][:, tok], in_=woven[i][:, tok, :].rearrange("p t j -> p (t j)")
+                )
+            for h in range(C // widths[i]):
+                c0 = widths[i] * h
+                b0 = c0 % BANK
+                nc.tensor.matmul_mx(
+                    out=z_ps[i][h][:],
+                    lhsT=xq[i][:].bitcast(FP8X4),
+                    lhsT_scale=xq_plane[i][:],
+                    rhs=wc[c0 // BANK][:, 2 * b0 : 2 * (b0 + widths[i])].bitcast(FP4X4),
+                    rhs_scale=wc_plane[:, c0 : c0 + widths[i]],
+                    start=True,
+                    stop=True,
+                )
+        for h in range(3):
+            nc.scalar.activation(out=z[0][:, 256 * h : 256 * (h + 1)], in_=z_ps[0][h][:], func=ACT.Copy)
+        nc.vector.tensor_copy(out=z[0][:, 768:1024], in_=z_ps[0][3][:])
+        for h in range(C // BANK):
+            nc.scalar.activation(out=z[1][:, BANK * h : BANK * (h + 1)], in_=z_ps[1][h][:], func=ACT.Copy)
+        for i in range(tiles):
+            nc.tensor.matmul_mx(
+                out=s_ps[i][:],
+                lhsT=xs[:, P * i : P * (i + 1)].bitcast(FP8X4),
+                lhsT_scale=xs_plane[:, P * i : P * (i + 1)],
+                rhs=ws[:].bitcast(FP4X4),
+                rhs_scale=ws_plane[:],
+                start=True,
+                stop=True,
+            )
+
+        def pick_rival(i, lo, hi):
+            nc.vector.tensor_copy(out=rival[i][:, lo:hi], in_=z[i][:].indirect(idx2[:, lo // LANES : hi // LANES]))
+
+        def pick_class(i, lo, hi):
+            nc.vector.tensor_tensor(out=margin[i][:, lo:hi], in0=z[i][:].indirect(idx[:, lo // LANES : hi // LANES]), in1=rival[i][:, lo:hi], op=ALU.subtract)
+            nc.scalar.activation(out=bent[i][:, lo:hi], in_=margin[i][:, lo:hi], func=ACT.Tanh)
+
+        def finish(i, lo, hi):
+            nc.vector.scalar_tensor_tensor(
+                out=res[i][:, lo:hi], in0=s_ps[i][:, lo:hi], scalar=0.5, in1=bent[i][:, lo:hi], op0=ALU.mult, op1=ALU.add
+            )
+            nc.sync.dma_start(out=out[P * i : P * (i + 1), lo:hi], in_=res[i][:, lo:hi])
+
+        pick_rival(0, 0, 256)
+        pick_rival(0, 256, 512)
+        pick_class(0, 0, 256)
+        pick_class(0, 256, 512)
+        pick_rival(1, 0, 256)
+        pick_rival(1, 256, 512)
+        finish(0, 0, 256)
+        pick_class(1, 0, 256)
+        pick_class(1, 256, 512)
+        finish(0, 256, 512)
+        finish(1, 0, 256)
+        finish(1, 256, 512)

@@ -37,7 +37,8 @@ def tile_list_class_and_its_rival_kernel(tc, xt, wc_words, wc_scales, xs_words, 
 
         idx = sb.tile([P, J // LANES], U16, name="idx")
         idx2 = sb.tile([P, J // LANES], U16, name="idx2")
-        wc = [sb.tile([P, 2 * BANK], U8, name=f"wc{h}", align_bytes=64) for h in range(C // BANK)]
+        wc_cuts = [0, 768, C]
+        wc = [sb.tile([P, 2 * (wc_cuts[h + 1] - wc_cuts[h])], U8, name=f"wc{h}", align_bytes=64) for h in range(2)]
         wc_plane = sb.tile([P, C], U8, name="wc_plane", align_bytes=64)
         xs = sb.tile([P, T], U32, name="xs", align_bytes=64)
         ws = sb.tile([P, 2 * J], U8, name="ws", align_bytes=64)
@@ -52,9 +53,8 @@ def tile_list_class_and_its_rival_kernel(tc, xt, wc_words, wc_scales, xs_words, 
         margin = [sb.tile([P, J], F32, name=f"margin{i}") for i in range(tiles)]
         bent = [sb.tile([P, J], F32, name=f"bent{i}") for i in range(tiles)]
         res = [sb.tile([P, J], F32, name=f"res{i}") for i in range(tiles)]
-        widths = [256, 512]
-        z_ps = [[ps.tile([P, widths[i]], F32, name=f"z_ps{i}_{h}") for h in range(C // widths[i])] for i in range(tiles)]
-        s_ps = [ps.tile([P, J], F32, name=f"s_ps{i}") for i in range(tiles)]
+        cuts = [[0,256,512,768,896,1024], [0,512,768,1024]]
+        z_ps = [[ps.tile([P, cuts[i][h + 1] - cuts[i][h]], F32, name=f"z_ps{i}_{h}", tag=f"bank{i}_{h}") for h in range(len(cuts[i]) - 1)] for i in range(tiles)]
 
         x_rows = xt.rearrange("(p j) t -> p j t", j=PACK)
         nc.vector.memset(wc_plane[:].bitcast(I32), 0)
@@ -63,9 +63,9 @@ def tile_list_class_and_its_rival_kernel(tc, xt, wc_words, wc_scales, xs_words, 
         wc_rows = wc_words[0].bitcast(I32)
         nc.sync.dma_start(out=raw[0][:], in_=x_rows[:, :, 0:P])
         load_scales([nc.scalar, nc.sync], wc_plane, wc_scales)
-        nc.sync.dma_start(out=wc[0][:].bitcast(I32), in_=wc_rows[:, 0 : BANK // 2])
+        nc.sync.dma_start(out=wc[0][:].bitcast(I32), in_=wc_rows[:, 0 : wc_cuts[1] // 2])
         nc.sync.dma_start(out=raw[1][:], in_=x_rows[:, :, P : 2 * P])
-        nc.sync.dma_start(out=wc[1][:].bitcast(I32), in_=wc_rows[:, BANK // 2 : BANK])
+        nc.sync.dma_start(out=wc[1][:].bitcast(I32), in_=wc_rows[:, wc_cuts[1] // 2 : C // 2])
         nc.sync.dma_start(idx2[:], offs2)
         nc.sync.dma_start(idx[:], offs)
         nc.sync.dma_start(out=ws[:].bitcast(I32), in_=ws_words[0].bitcast(I32))
@@ -84,23 +84,27 @@ def tile_list_class_and_its_rival_kernel(tc, xt, wc_words, wc_scales, xs_words, 
                 nc.vector.quantize_mx(
                     out=xq[i][:, tok].bitcast(FP8X4), scales=xq_plane[i][:, tok], in_=woven[i][:, tok, :].rearrange("p t j -> p (t j)")
                 )
-            for h in range(C // widths[i]):
-                c0 = widths[i] * h
-                b0 = c0 % BANK
+            for h in range(len(cuts[i]) - 1):
+                c0, c1 = cuts[i][h], cuts[i][h + 1]
+                part = 0 if c0 < wc_cuts[1] else 1
+                b0 = c0 - wc_cuts[part]
                 nc.tensor.matmul_mx(
                     out=z_ps[i][h][:],
                     lhsT=xq[i][:].bitcast(FP8X4),
                     lhsT_scale=xq_plane[i][:],
-                    rhs=wc[c0 // BANK][:, 2 * b0 : 2 * (b0 + widths[i])].bitcast(FP4X4),
-                    rhs_scale=wc_plane[:, c0 : c0 + widths[i]],
+                    rhs=wc[part][:, 2 * b0 : 2 * (b0 + c1 - c0)].bitcast(FP4X4),
+                    rhs_scale=wc_plane[:, c0:c1],
                     start=True,
                     stop=True,
                 )
-        for h in range(3):
-            nc.scalar.activation(out=z[0][:, 256 * h : 256 * (h + 1)], in_=z_ps[0][h][:], func=ACT.Copy)
-        nc.vector.tensor_copy(out=z[0][:, 768:1024], in_=z_ps[0][3][:])
-        for h in range(C // BANK):
-            nc.scalar.activation(out=z[1][:, BANK * h : BANK * (h + 1)], in_=z_ps[1][h][:], func=ACT.Copy)
+        for i in range(tiles):
+            for h in range(len(cuts[i]) - 1):
+                cols = slice(cuts[i][h], cuts[i][h + 1])
+                if i == 0 and h >= 3:
+                    nc.vector.tensor_copy(out=z[i][:, cols], in_=z_ps[i][h][:])
+                else:
+                    nc.scalar.activation(out=z[i][:, cols], in_=z_ps[i][h][:], func=ACT.Copy)
+        s_ps = [ps.tile([P, J], F32, name=f"s_ps{i}", tag=f"bank0_{i}") for i in range(tiles)]
         for i in range(tiles):
             nc.tensor.matmul_mx(
                 out=s_ps[i][:],

from contextlib import ExitStack

import concourse.mybir as mybir

K, L, T, C, J = 512, 512, 256, 1024, 512
FLOPS = 2 * K * T * C + 2 * L * T * J

F32 = mybir.dt.float32
BF16 = mybir.dt.bfloat16
I32 = mybir.dt.int32
U32 = mybir.dt.uint32
U16 = mybir.dt.uint16
U8 = mybir.dt.uint8
FP8X4 = mybir.dt.float8_e4m3fn_x4
FP4X4 = mybir.dt.float4_e2m1fn_x4
ALU = mybir.AluOpType
ACT = mybir.ActivationFunctionType

P = 128
PACK = 4
BANK = 512
PIECE = 256
LANES = 16


def load_scales(engines, plane, scales):
    for q in range(4):
        engines[q % len(engines)].dma_start(out=plane[32 * q : 32 * q + 4, :].bitcast(I32), in_=scales[0, 4 * q : 4 * q + 4, :].bitcast(I32))


def tile_list_class_and_its_rival_kernel(tc, xt, wc_words, wc_scales, xs_words, xs_scales, ws_words, ws_scales, offs, offs2, out):
    nc = tc.nc
    tiles = T // P
    with ExitStack() as ctx:
        sb = ctx.enter_context(tc.tile_pool(name="sb", bufs=1))
        ps = ctx.enter_context(tc.psum_pool(name="ps", bufs=1))

        idx = sb.tile([P, J // LANES], U16, name="idx")
        idx2 = sb.tile([P, J // LANES], U16, name="idx2")
        wc_cuts = [0, 768, C]
        wc = [sb.tile([P, 2 * (wc_cuts[h + 1] - wc_cuts[h])], U8, name=f"wc{h}", align_bytes=64) for h in range(2)]
        wc_plane = sb.tile([P, C], U8, name="wc_plane", align_bytes=64)
        xs = sb.tile([P, T], U32, name="xs", align_bytes=64)
        ws = sb.tile([P, 2 * J], U8, name="ws", align_bytes=64)
        xs_plane = sb.tile([P, T], U8, name="xs_plane", align_bytes=64)
        ws_plane = sb.tile([P, J], U8, name="ws_plane", align_bytes=64)
        raw = [sb.tile([P, PACK, P], F32, name=f"raw{i}") for i in range(tiles)]
        woven = [sb.tile([P, P, PACK], BF16, name=f"woven{i}", align_bytes=64) for i in range(tiles)]
        xq = [sb.tile([P, P], U32, name=f"xq{i}", align_bytes=64) for i in range(tiles)]
        xq_plane = [sb.tile([P, P], U8, name=f"xq_plane{i}", align_bytes=64) for i in range(tiles)]
        z = [sb.tile([P, C], F32, name=f"z{i}") for i in range(tiles)]
        rival = [sb.tile([P, J], F32, name=f"rival{i}") for i in range(tiles)]
        margin = [sb.tile([P, J], F32, name=f"margin{i}") for i in range(tiles)]
        bent = [sb.tile([P, J], F32, name=f"bent{i}") for i in range(tiles)]
        res = [sb.tile([P, J], F32, name=f"res{i}") for i in range(tiles)]
        cuts = [[0,256,512,768,896,1024], [0,512,768,1024]]
        z_ps = [[ps.tile([P, cuts[i][h + 1] - cuts[i][h]], F32, name=f"z_ps{i}_{h}", tag=f"bank{i}_{h}") for h in range(len(cuts[i]) - 1)] for i in range(tiles)]

        x_rows = xt.rearrange("(p j) t -> p j t", j=PACK)
        nc.vector.memset(wc_plane[:].bitcast(I32), 0)
        nc.vector.memset(ws_plane[:].bitcast(I32), 0)
        nc.vector.memset(xs_plane[:].bitcast(I32), 0)
        wc_rows = wc_words[0].bitcast(I32)
        nc.sync.dma_start(out=raw[0][:], in_=x_rows[:, :, 0:P])
        load_scales([nc.scalar, nc.sync], wc_plane, wc_scales)
        nc.sync.dma_start(out=wc[0][:].bitcast(I32), in_=wc_rows[:, 0 : wc_cuts[1] // 2])
        nc.sync.dma_start(out=raw[1][:], in_=x_rows[:, :, P : 2 * P])
        nc.sync.dma_start(out=wc[1][:].bitcast(I32), in_=wc_rows[:, wc_cuts[1] // 2 : C // 2])
        nc.sync.dma_start(idx2[:], offs2)
        nc.sync.dma_start(idx[:], offs)
        nc.sync.dma_start(out=ws[:].bitcast(I32), in_=ws_words[0].bitcast(I32))
        nc.sync.dma_start(out=xs[:].bitcast(I32), in_=xs_words[0].rearrange("p c r -> p (c r)").bitcast(I32))
        load_scales([nc.sync], ws_plane, ws_scales)
        load_scales([nc.sync], xs_plane, xs_scales)

        for i in range(tiles):
            halves = [slice(0, P // 2), slice(P // 2, P)] if i == 0 else [slice(0, P)]
            for tok in halves:
                nc.vector.tensor_copy(
                    out=woven[i][:, tok, :].rearrange("p (c e) j -> p c j e", e=4),
                    in_=raw[i][:, :, tok].rearrange("p j (c e) -> p c j e", e=4),
                )
            for tok in halves:
                nc.vector.quantize_mx(
                    out=xq[i][:, tok].bitcast(FP8X4), scales=xq_plane[i][:, tok], in_=woven[i][:, tok, :].rearrange("p t j -> p (t j)")
                )
            for h in range(len(cuts[i]) - 1):
                c0, c1 = cuts[i][h], cuts[i][h + 1]
                part = 0 if c0 < wc_cuts[1] else 1
                b0 = c0 - wc_cuts[part]
                nc.tensor.matmul_mx(
                    out=z_ps[i][h][:],
                    lhsT=xq[i][:].bitcast(FP8X4),
                    lhsT_scale=xq_plane[i][:],
                    rhs=wc[part][:, 2 * b0 : 2 * (b0 + c1 - c0)].bitcast(FP4X4),
                    rhs_scale=wc_plane[:, c0:c1],
                    start=True,
                    stop=True,
                )
        for i in range(tiles):
            for h in range(len(cuts[i]) - 1):
                cols = slice(cuts[i][h], cuts[i][h + 1])
                if i == 0 and h >= 3:
                    nc.vector.tensor_copy(out=z[i][:, cols], in_=z_ps[i][h][:])
                else:
                    nc.scalar.activation(out=z[i][:, cols], in_=z_ps[i][h][:], func=ACT.Copy)
        s_ps = [ps.tile([P, J], F32, name=f"s_ps{i}", tag=f"bank0_{i}") for i in range(tiles)]
        for i in range(tiles):
            nc.tensor.matmul_mx(
                out=s_ps[i][:],
                lhsT=xs[:, P * i : P * (i + 1)].bitcast(FP8X4),
                lhsT_scale=xs_plane[:, P * i : P * (i + 1)],
                rhs=ws[:].bitcast(FP4X4),
                rhs_scale=ws_plane[:],
                start=True,
                stop=True,
            )

        def pick_rival(i, lo, hi):
            nc.vector.tensor_copy(out=rival[i][:, lo:hi], in_=z[i][:].indirect(idx2[:, lo // LANES : hi // LANES]))

        def pick_class(i, lo, hi):
            nc.vector.tensor_tensor(out=margin[i][:, lo:hi], in0=z[i][:].indirect(idx[:, lo // LANES : hi // LANES]), in1=rival[i][:, lo:hi], op=ALU.subtract)
            nc.scalar.activation(out=bent[i][:, lo:hi], in_=margin[i][:, lo:hi], func=ACT.Tanh)

        def finish(i, lo, hi):
            nc.vector.scalar_tensor_tensor(
                out=res[i][:, lo:hi], in0=s_ps[i][:, lo:hi], scalar=0.5, in1=bent[i][:, lo:hi], op0=ALU.mult, op1=ALU.add
            )
            nc.sync.dma_start(out=out[P * i : P * (i + 1), lo:hi], in_=res[i][:, lo:hi])

        pick_rival(0, 0, 256)
        pick_rival(0, 256, 512)
        pick_class(0, 0, 256)
        pick_class(0, 256, 512)
        pick_rival(1, 0, 256)
        pick_rival(1, 256, 512)
        finish(0, 0, 256)
        pick_class(1, 0, 256)
        pick_class(1, 256, 512)
        finish(0, 256, 512)
        finish(1, 0, 256)
        finish(1, 256, 512)
